import numpy as np
import ml_dtypes


def mxq(x, axis, fmt="e4m3"):
    dtype, down = {"e4m3": (ml_dtypes.float8_e4m3fn, 7), "e5m2": (ml_dtypes.float8_e5m2, 14)}[fmt]
    v = np.moveaxis(np.asarray(x, np.float32).astype(ml_dtypes.bfloat16).astype(np.float64), axis, -1)
    blocks = v.reshape(v.shape[:-1] + (-1, 32))
    amax = np.abs(blocks).max(-1, keepdims=True)
    byte = np.maximum(np.where(amax > 0, np.frexp(amax)[1] - 1 + 127, 0) - down, 1)
    scale = np.exp2(byte - 127.0)
    codes = (blocks / scale).astype(np.float32).astype(dtype).astype(np.float64)
    return np.moveaxis((codes * scale).reshape(v.shape), -1, axis)


WIDE = False


def mx_kscale(k):
    if not WIDE:
        return np.ones(k)
    levels = np.array([30, -30])
    if k % 512:
        return np.exp2(np.random.permutation(np.resize(levels, k // 32))).repeat(32)
    a = np.empty((k // 512, 16))
    for p in range(k // 512):
        a[p, :8] = np.random.permutation(np.resize(levels, 8))
        for g in range(8):
            far = levels[np.abs(levels - a[p, g]) >= 10]
            a[p, g + 8] = far[np.random.randint(len(far))]
    return np.exp2(a.ravel()).repeat(32)


def f64(x):
    return np.asarray(x).astype(np.float64)


def striped(idx):
    return np.tile(np.asarray(idx).reshape(-1, 16).T, (8, 1)).astype(np.uint16)


def unstriped(offs):
    return offs[:16].T.reshape(-1).astype(np.int64)


E2M1 = np.array([0.0, 0.5, 1.0, 1.5, 2.0, 3.0, 4.0, 6.0, -0.0, -0.5, -1.0, -1.5, -2.0, -3.0, -4.0, -6.0])


def pack_weight(w, fmt):
    k, n = w.shape
    w = f64(np.asarray(w, np.float32).astype(ml_dtypes.bfloat16)).reshape(k // 32, 32, n)
    amax = np.abs(w).max(1)
    if fmt in ("e4m3", "e5m2"):
        byte = np.frexp(amax)[1] - 1 + 127 - (7 if fmt == "e4m3" else 14)
    else:
        mant, ex = np.frexp(amax / 6.0)
        byte = np.where(mant > 0.5, ex, ex - 1) + 127
    byte = np.clip(np.where(amax > 0, byte, 1), 1, 254)
    scaled = (w * np.exp2(127.0 - byte)[:, None, :]).reshape(k, n).astype(np.float32)
    by_word = np.ascontiguousarray(scaled.reshape(k // 512, 128, 4, n).transpose(0, 1, 3, 2))
    if fmt in ("e4m3", "e5m2"):
        words = by_word.astype(ml_dtypes.float8_e4m3fn if fmt == "e4m3" else ml_dtypes.float8_e5m2).view(np.uint8)
    else:
        c = by_word.astype(ml_dtypes.float4_e2m1fn).view(np.uint8) & 0xF
        words = (c[..., 0::2] | (c[..., 1::2] << 4)).reshape(k // 512, 128, 2 * n)
    return np.ascontiguousarray(words), np.ascontiguousarray(byte.astype(np.uint8).reshape(k // 512, 16, n))


def unpack_weight(words, scales, fmt):
    g, _, n = scales.shape
    words = np.ascontiguousarray(words).reshape(g, 128, n, -1)
    if fmt in ("e4m3", "e5m2"):
        vals = words.view(ml_dtypes.float8_e4m3fn if fmt == "e4m3" else ml_dtypes.float8_e5m2).astype(np.float64)
    else:
        nib = np.empty((g, 128, n, 4), np.uint8)
        nib[..., 0::2] = words & 0xF
        nib[..., 1::2] = words >> 4
        vals = E2M1[nib]
    vals = vals * np.repeat(np.exp2(scales.astype(np.float64) - 127.0), 8, axis=1)[..., None]
    return vals.transpose(0, 1, 3, 2).reshape(g * 512, n)


K, T, J, I, R, G, S = 512, 512, 256, 256, 512, 32, 32


def setup_inputs():
    n = np.random.standard_normal
    idx = np.random.permutation(T)[:J]
    idx2 = np.random.permutation(T)[:I]
    fk = mx_kscale(K)
    fr = mx_kscale(R)
    xtp = pack_weight(n((K, T)) / fk[:, None], "e4m3")
    wap = pack_weight(n((K, R)) * 0.5 / np.sqrt(K) * fk[:, None] * fr, "e2m1")
    wbp = pack_weight(n((K, R)) * 1 / np.sqrt(K) * fk[:, None] / fr, "e5m2")
    return {
        "xt_words": xtp[0],
        "xt_scales": xtp[1],
        "wa_words": wap[0],
        "wa_scales": wap[1],
        "wb_words": wbp[0],
        "wb_scales": wbp[1],
        "bi": (np.random.uniform(-15.0, 15.0, (1, I))).astype(np.float32),
        "offs": striped(idx),
        "offs2": striped(idx2),
    }


def reference(xt_words, xt_scales, wa_words, wa_scales, wb_words, wb_scales, bi, offs, offs2):
    idx = unstriped(offs)
    idx2 = unstriped(offs2)
    xtu = unpack_weight(xt_words, xt_scales, "e4m3")
    wau = unpack_weight(wa_words, wa_scales, "e2m1")
    wbu = unpack_weight(wb_words, wb_scales, "e5m2")
    xtidxg = xtu[:, idx]
    za = wau.T @ xtidxg
    ya1 = np.pad(za, ((0, 0), (1, 0)))[:, :J]
    ha = za - 0.6 * ya1
    xtidx2g = xtu[:, idx2]
    zb = wbu.T @ xtidx2g
    mb1 = zb.reshape(R, G, I // G).mean(axis=2)
    mb2 = np.repeat(mb1, I // G, axis=1)
    hb = zb - mb2
    haq = mxq(ha, 0, "e4m3")
    hbq = mxq(hb, 0, "e5m2")
    a0 = haq.T @ hbq
    a = a0 + f64(bi)
    g1 = a.reshape(J, S, I // S).max(axis=2)
    y = 0.04 * g1
    return y

@@ -1,0 +1,202 @@
+from contextlib import ExitStack
+
+import concourse.mybir as mybir
+
+K, T, J, I, R, G, S = 512, 512, 256, 256, 512, 32, 32
+FLOPS = 2 * K * R * J + 2 * K * R * I + 2 * R * J * I
+
+F32 = mybir.dt.float32
+BF16 = mybir.dt.bfloat16
+I32 = mybir.dt.int32
+U32 = mybir.dt.uint32
+U16 = mybir.dt.uint16
+U8 = mybir.dt.uint8
+E4M3 = mybir.dt.float8_e4m3fn_x4
+E5M2 = mybir.dt.float8_e5m2_x4
+E2M1 = mybir.dt.float4_e2m1fn_x4
+ALU = mybir.AluOpType
+
+P = 128
+PACK = 4
+HALF = 128
+RUN = 8
+
+
+def load_scale_rows(queues, tile, scales):
+    for quadrant, queue in enumerate(queues):
+        queue.dma_start(
+            out=tile[32 * quadrant : 32 * quadrant + 4, :].bitcast(I32),
+            in_=scales[0, 4 * quadrant : 4 * quadrant + 4, :].bitcast(I32),
+        )
+
+
+def deal_columns(nc, dealt, raw, run):
+    nc.scalar.copy(
+        out=dealt.rearrange("p (t b q) -> p t b q", t=PACK, q=run),
+        in_=raw.rearrange("p (b t q) -> p t b q", t=PACK, q=run),
+    )
+
+
+def tile_list_meet_lagged_levelled_bundlemax_kernel(
+    tc, xt_words, xt_scales, wa_words, wa_scales, wb_words, wb_scales, bi, offs, offs2, out
+):
+    nc = tc.nc
+    with ExitStack() as ctx:
+        sb = ctx.enter_context(tc.tile_pool(name="sb", bufs=1))
+        ps = ctx.enter_context(tc.psum_pool(name="ps", bufs=1))
+
+        rows_list = sb.tile([P, J // 16], U16, name="rows_list")
+        cols_list = sb.tile([P, I // 16], U16, name="cols_list")
+        x_words = sb.tile([P, T], U32, name="x_words", align_bytes=64)
+        x_scales = sb.tile([P, T], U8, name="x_scales", align_bytes=64)
+        wa_raw = sb.tile([P, R], U16, name="wa_raw", align_bytes=64)
+        wa_raw_scales = sb.tile([P, R], U8, name="wa_raw_scales", align_bytes=64)
+        wb_raw = sb.tile([P, R], U32, name="wb_raw", align_bytes=64)
+        wb_raw_scales = sb.tile([P, R], U8, name="wb_raw_scales", align_bytes=64)
+        bias = sb.tile([P, I], F32, name="bias", align_bytes=64)
+        za = sb.tile([P, (1 + J) * PACK], F32, name="za", align_bytes=64)
+
+        nc.vector.memset(x_scales[:].bitcast(I32), 0)
+        nc.vector.memset(wb_raw_scales[:].bitcast(I32), 0)
+        nc.vector.memset(wa_raw_scales[:].bitcast(I32), 0)
+        nc.vector.memset(za[:, 0:PACK], 0.0)
+
+        nc.sync.dma_start(cols_list[:], offs2)
+        nc.sync.dma_start(out=x_words[:].bitcast(I32), in_=xt_words[0].rearrange("p n t -> p (n t)").bitcast(I32))
+        load_scale_rows([nc.scalar] * 4, x_scales, xt_scales)
+        nc.sync.dma_start(out=wb_raw[:].bitcast(I32), in_=wb_words[0].rearrange("p n t -> p (n t)").bitcast(I32))
+        nc.sync.dma_start(rows_list[:], offs)
+        load_scale_rows([nc.sync] * 4, wb_raw_scales, wb_scales)
+        nc.sync.dma_start(out=wa_raw[:].bitcast(I32), in_=wa_words[0].bitcast(I32))
+        load_scale_rows([nc.sync, nc.sync, nc.gpsimd, nc.gpsimd], wa_raw_scales, wa_scales)
+        nc.sync.dma_start(out=bias[:], in_=bi[0].partition_broadcast(P))
+
+        xb_words = sb.tile([P, I], U32, name="xb_words", align_bytes=64)
+        xb_scales = sb.tile([P, I], U8, name="xb_scales", align_bytes=64)
+        xa_words = sb.tile([P, J], U32, name="xa_words", align_bytes=64)
+        xa_scales = sb.tile([P, J], U8, name="xa_scales", align_bytes=64)
+        nc.vector.tensor_copy(xb_words[:], x_words[:].indirect(cols_list[:]))
+        nc.vector.tensor_copy(xb_scales[:], x_scales[:].indirect(cols_list[:]))
+        nc.vector.tensor_copy(xa_words[:], x_words[:].indirect(rows_list[:]))
+        nc.vector.tensor_copy(xa_scales[:], x_scales[:].indirect(rows_list[:]))
+
+        wb_dealt = sb.tile([P, R], U32, name="wb_dealt", align_bytes=64)
+        wb_dealt_scales = sb.tile([P, R], U8, name="wb_dealt_scales", align_bytes=64)
+        wa_dealt = sb.tile([P, R], U16, name="wa_dealt", align_bytes=64)
+        wa_dealt_scales = sb.tile([P, R], U8, name="wa_dealt_scales", align_bytes=64)
+        deal_columns(nc, wb_dealt[:], wb_raw[:], RUN)
+        deal_columns(nc, wb_dealt_scales[:].bitcast(U32), wb_raw_scales[:].bitcast(U32), RUN // 4)
+        deal_columns(nc, wa_dealt[:].bitcast(U32), wa_raw[:].bitcast(U32), RUN // 2)
+        deal_columns(nc, wa_dealt_scales[:].bitcast(U32), wa_raw_scales[:].bitcast(U32), RUN // 4)
+
+        zb_banks = [ps.tile([P, PACK, HALF], F32, name="zb_bank%d" % h) for h in range(2)]
+        za_banks = [ps.tile([P, PACK, HALF], F32, name="za_bank%d" % h) for h in range(2)]
+        for h in range(2):
+            cols = slice(h * HALF, (h + 1) * HALF)
+            for t in range(PACK):
+                feats = slice(t * P, (t + 1) * P)
+                nc.tensor.matmul_mx(
+                    out=zb_banks[h][:, t, :],
+                    lhsT=wb_dealt[:, feats].bitcast(E5M2),
+                    lhsT_scale=wb_dealt_scales[:, feats],
+                    rhs=xb_words[:, cols].bitcast(E4M3),
+                    rhs_scale=xb_scales[:, cols],
+                    start=True,
+                    stop=True,
+                )
+        for h in range(2):
+            rows = slice(h * HALF, (h + 1) * HALF)
+            for t in range(PACK):
+                feats = slice(t * P, (t + 1) * P)
+                nc.tensor.matmul_mx(
+                    out=za_banks[h][:, t, :],
+                    lhsT=wa_dealt[:, feats].bitcast(E2M1),
+                    lhsT_scale=wa_dealt_scales[:, feats],
+                    rhs=xa_words[:, rows].bitcast(E4M3),
+                    rhs_scale=xa_scales[:, rows],
+                    start=True,
+                    stop=True,
+                )
+            nc.scalar.copy(
+                out=za[:, (1 + h * HALF) * PACK : (1 + (h + 1) * HALF) * PACK].rearrange("p (j t) -> p j t", t=PACK),
+                in_=za_banks[h][:].rearrange("p t j -> p j t"),
+            )
+
+        scaled_bias = sb.tile([P, I], F32, name="scaled_bias", align_bytes=64)
+        nc.gpsimd.tensor_scalar(scaled_bias[:], bias[:], 0.04, 0.0, ALU.mult, ALU.add)
+
+        bundles = HALF // RUN
+        sums = [sb.tile([P, bundles, PACK], F32, name="sums%d" % h) for h in range(2)]
+        means = [sb.tile([P, bundles, 1, PACK], F32, name="means%d" % h) for h in range(2)]
+        hb = sb.tile([P, I * PACK], BF16, name="hb", align_bytes=64)
+        ha = [sb.tile([P, HALF * PACK], BF16, name="ha%d" % h, align_bytes=64) for h in range(2)]
+        for h in range(2):
+            nc.vector.tensor_reduce(
+                out=sums[h][:],
+                in_=zb_banks[h][:].rearrange("p t (g m) -> p g t m", m=RUN),
+                axis=mybir.AxisListType.X,
+                op=ALU.add,
+            )
+        for h in range(2):
+            nc.vector.tensor_scalar(means[h][:, :, 0, :], sums[h][:], 1.0 / RUN, None, ALU.mult)
+        for h in range(2):
+            nc.vector.tensor_tensor(
+                out=hb[:, h * HALF * PACK : (h + 1) * HALF * PACK].rearrange("p (g m t) -> p g m t", m=RUN, t=PACK),
+                in0=zb_banks[h][:].rearrange("p t (g m) -> p g m t", m=RUN),
+                in1=means[h][:].broadcast_to([P, bundles, RUN, PACK]),
+                op=ALU.subtract,
+            )
+
+        def lag(h):
+            nc.vector.scalar_tensor_tensor(
+                out=ha[h][:].rearrange("p (j t) -> p j t", t=PACK),
+                in0=za[:, h * HALF * PACK : (h + 1) * HALF * PACK].rearrange("p (j t) -> p j t", t=PACK),
+                scalar=-0.6,
+                in1=za_banks[h][:].rearrange("p t j -> p j t"),
+                op0=ALU.mult,
+                op1=ALU.add,
+            )
+
+        hb_codes = sb.tile([P, I], U32, name="hb_codes", align_bytes=64)
+        hb_scales = sb.tile([P, I], U8, name="hb_scales", align_bytes=64)
+        ha_codes = [sb.tile([P, HALF], U32, name="ha_codes%d" % h, align_bytes=64) for h in range(2)]
+        ha_scales = [sb.tile([P, HALF], U8, name="ha_scales%d" % h, align_bytes=64) for h in range(2)]
+        a_banks = [ps.tile([P, I], F32, name="a_bank%d" % h) for h in range(2)]
+        scores = [sb.tile([P, I], F32, name="scores%d" % h, align_bytes=64) for h in range(2)]
+        best = [sb.tile([P, S], F32, name="best%d" % h, align_bytes=64) for h in range(2)]
+
+        def meet(h):
+            nc.vector.quantize_mx(out=ha_codes[h][:].bitcast(E4M3), scales=ha_scales[h][:], in_=ha[h][:])
+            nc.tensor.matmul_mx(
+                out=a_banks[h][:],
+                lhsT=ha_codes[h][:].bitcast(E4M3),
+                lhsT_scale=ha_scales[h][:],
+                rhs=hb_codes[:].bitcast(E5M2),
+                rhs_scale=hb_scales[:],
+                start=True,
+                stop=True,
+            )
+
+        def add_bias(h):
+            nc.vector.scalar_tensor_tensor(
+                out=scores[h][:], in0=a_banks[h][:], scalar=0.04, in1=scaled_bias[:], op0=ALU.mult, op1=ALU.add
+            )
+
+        def keep_best(h):
+            nc.vector.tensor_reduce(
+                out=best[h][:],
+                in_=scores[h][:].rearrange("p (s m) -> p s m", m=I // S),
+                axis=mybir.AxisListType.X,
+                op=ALU.max,
+            )
+            nc.sync.dma_start(out=out[h * HALF : (h + 1) * HALF, :], in_=best[h][:])
+
+        lag(0)
+        nc.vector.quantize_mx(out=hb_codes[:].bitcast(E5M2), scales=hb_scales[:], in_=hb[:])
+        meet(0)
+        lag(1)
+        add_bias(0)
+        meet(1)
+        keep_best(0)
+        add_bias(1)
+        keep_best(1)

@@ -50,7 +50,7 @@ def tile_list_meet_lagged_levelled_bundlemax_kernel(
         x_words = sb.tile([P, T], U32, name="x_words", align_bytes=64)
         x_scales = sb.tile([P, T], U8, name="x_scales", align_bytes=64)
         wa_raw = sb.tile([P, R], U16, name="wa_raw", align_bytes=64)
-        wa_raw_scales = sb.tile([P, R], U8, name="wa_raw_scales", align_bytes=64)
+        wa_raw_scales = sb.tile([P, R], U8, name="wa_raw_scales", tag="wa_raw_scales", align_bytes=64)
         wb_raw = sb.tile([P, R], U32, name="wb_raw", align_bytes=64)
         wb_raw_scales = sb.tile([P, R], U8, name="wb_raw_scales", align_bytes=64)
         bias = sb.tile([P, I], F32, name="bias", align_bytes=64)
@@ -62,10 +62,10 @@ def tile_list_meet_lagged_levelled_bundlemax_kernel(
         nc.vector.memset(za[:, 0:PACK], 0.0)
 
         nc.sync.dma_start(cols_list[:], offs2)
+        nc.sync.dma_start(rows_list[:], offs)
         nc.sync.dma_start(out=x_words[:].bitcast(I32), in_=xt_words[0].rearrange("p n t -> p (n t)").bitcast(I32))
         load_scale_rows([nc.scalar] * 4, x_scales, xt_scales)
         nc.sync.dma_start(out=wb_raw[:].bitcast(I32), in_=wb_words[0].rearrange("p n t -> p (n t)").bitcast(I32))
-        nc.sync.dma_start(rows_list[:], offs)
         load_scale_rows([nc.sync] * 4, wb_raw_scales, wb_scales)
         nc.sync.dma_start(out=wa_raw[:].bitcast(I32), in_=wa_words[0].bitcast(I32))
         load_scale_rows([nc.sync, nc.sync, nc.gpsimd, nc.gpsimd], wa_raw_scales, wa_scales)
@@ -82,7 +82,7 @@ def tile_list_meet_lagged_levelled_bundlemax_kernel(
 
         wb_dealt = sb.tile([P, R], U32, name="wb_dealt", align_bytes=64)
         wb_dealt_scales = sb.tile([P, R], U8, name="wb_dealt_scales", align_bytes=64)
-        wa_dealt = sb.tile([P, R], U16, name="wa_dealt", align_bytes=64)
+        wa_dealt = sb.tile([P, R], U16, name="wa_dealt", tag="wa_dealt", align_bytes=64)
         wa_dealt_scales = sb.tile([P, R], U8, name="wa_dealt_scales", align_bytes=64)
         deal_columns(nc, wb_dealt[:], wb_raw[:], RUN)
         deal_columns(nc, wb_dealt_scales[:].bitcast(U32), wb_raw_scales[:].bitcast(U32), RUN // 4)
@@ -104,6 +104,20 @@ def tile_list_meet_lagged_levelled_bundlemax_kernel(
                     start=True,
                     stop=True,
                 )
+        bundles = HALF // RUN
+        sums = [sb.tile([P, bundles, PACK], F32, name="sums%d" % h) for h in range(2)]
+        means = [sb.tile([P, bundles, 1, PACK], F32, name="means%d" % h) for h in range(2)]
+        hb = sb.tile([P, I * PACK], BF16, name="hb", align_bytes=64)
+        ha = [sb.tile([P, HALF * PACK], BF16, name="ha%d" % h, align_bytes=64) for h in range(2)]
+        for h in range(2):
+            nc.vector.tensor_reduce(
+                out=sums[h][:],
+                in_=zb_banks[h][:].rearrange("p t (g m) -> p g t m", m=RUN),
+                axis=mybir.AxisListType.X,
+                op=ALU.add,
+            )
+        zb_late = sb.tile([P, HALF, PACK], F32, name="zb_late", tag="wa_raw_scales", align_bytes=64)
+        nc.scalar.copy(out=zb_late[:], in_=zb_banks[0][:].rearrange("p t i -> p i t"))
         for h in range(2):
             rows = slice(h * HALF, (h + 1) * HALF)
             for t in range(PACK):
@@ -122,27 +136,20 @@ def tile_list_meet_lagged_levelled_bundlemax_kernel(
                 in_=za_banks[h][:].rearrange("p t j -> p j t"),
             )
 
-        scaled_bias = sb.tile([P, I], F32, name="scaled_bias", align_bytes=64)
-        nc.gpsimd.tensor_scalar(scaled_bias[:], bias[:], 0.04, 0.0, ALU.mult, ALU.add)
+        scaled_bias = sb.tile([P, I], F32, name="scaled_bias", tag="wa_dealt", align_bytes=64)
+        nc.scalar.activation(out=scaled_bias[:], in_=bias[:], func=mybir.ActivationFunctionType.Copy, scale=0.04)
 
-        bundles = HALF // RUN
-        sums = [sb.tile([P, bundles, PACK], F32, name="sums%d" % h) for h in range(2)]
-        means = [sb.tile([P, bundles, 1, PACK], F32, name="means%d" % h) for h in range(2)]
-        hb = sb.tile([P, I * PACK], BF16, name="hb", align_bytes=64)
-        ha = [sb.tile([P, HALF * PACK], BF16, name="ha%d" % h, align_bytes=64) for h in range(2)]
-        for h in range(2):
-            nc.vector.tensor_reduce(
-                out=sums[h][:],
-                in_=zb_banks[h][:].rearrange("p t (g m) -> p g t m", m=RUN),
-                axis=mybir.AxisListType.X,
-                op=ALU.add,
-            )
-        for h in range(2):
-            nc.vector.tensor_scalar(means[h][:, :, 0, :], sums[h][:], 1.0 / RUN, None, ALU.mult)
-        for h in range(2):
-            nc.vector.tensor_tensor(
+        nc.gpsimd.tensor_scalar(means[0][:, :, 0, :], sums[0][:], 1.0 / RUN, 0.0, ALU.mult, ALU.add)
+        nc.vector.tensor_scalar(means[1][:, :, 0, :], sums[1][:], 1.0 / RUN, None, ALU.mult)
+        zb_views = [
+            zb_late[:].rearrange("p (g m) t -> p g m t", m=RUN),
+            zb_banks[1][:].rearrange("p t (g m) -> p g m t", m=RUN),
+        ]
+
+        def level(h, engine):
+            engine.tensor_tensor(
                 out=hb[:, h * HALF * PACK : (h + 1) * HALF * PACK].rearrange("p (g m t) -> p g m t", m=RUN, t=PACK),
-                in0=zb_banks[h][:].rearrange("p t (g m) -> p g m t", m=RUN),
+                in0=zb_views[h],
                 in1=means[h][:].broadcast_to([P, bundles, RUN, PACK]),
                 op=ALU.subtract,
             )
@@ -165,8 +172,10 @@ def tile_list_meet_lagged_levelled_bundlemax_kernel(
         scores = [sb.tile([P, I], F32, name="scores%d" % h, align_bytes=64) for h in range(2)]
         best = [sb.tile([P, S], F32, name="best%d" % h, align_bytes=64) for h in range(2)]
 
-        def meet(h):
+        def quantize_rows(h):
             nc.vector.quantize_mx(out=ha_codes[h][:].bitcast(E4M3), scales=ha_scales[h][:], in_=ha[h][:])
+
+        def meet(h):
             nc.tensor.matmul_mx(
                 out=a_banks[h][:],
                 lhsT=ha_codes[h][:].bitcast(E4M3),
@@ -191,12 +200,16 @@ def tile_list_meet_lagged_levelled_bundlemax_kernel(
             )
             nc.sync.dma_start(out=out[h * HALF : (h + 1) * HALF, :], in_=best[h][:])
 
+        level(0, nc.gpsimd)
         lag(0)
+        level(1, nc.vector)
+        lag(1)
+        quantize_rows(0)
         nc.vector.quantize_mx(out=hb_codes[:].bitcast(E5M2), scales=hb_scales[:], in_=hb[:])
         meet(0)
-        lag(1)
-        add_bias(0)
+        quantize_rows(1)
         meet(1)
-        keep_best(0)
+        add_bias(0)
         add_bias(1)
+        keep_best(0)
         keep_best(1)

@@ -66,9 +66,9 @@ def tile_list_meet_lagged_levelled_bundlemax_kernel(
         nc.sync.dma_start(out=x_words[:].bitcast(I32), in_=xt_words[0].rearrange("p n t -> p (n t)").bitcast(I32))
         load_scale_rows([nc.scalar] * 4, x_scales, xt_scales)
         nc.sync.dma_start(out=wb_raw[:].bitcast(I32), in_=wb_words[0].rearrange("p n t -> p (n t)").bitcast(I32))
-        load_scale_rows([nc.sync] * 4, wb_raw_scales, wb_scales)
+        load_scale_rows([nc.sync, nc.sync, nc.sync, nc.gpsimd], wb_raw_scales, wb_scales)
         nc.sync.dma_start(out=wa_raw[:].bitcast(I32), in_=wa_words[0].bitcast(I32))
-        load_scale_rows([nc.sync, nc.sync, nc.gpsimd, nc.gpsimd], wa_raw_scales, wa_scales)
+        load_scale_rows([nc.sync, nc.sync, nc.sync, nc.gpsimd], wa_raw_scales, wa_scales)
         nc.sync.dma_start(out=bias[:], in_=bi[0].partition_broadcast(P))
 
         xb_words = sb.tile([P, I], U32, name="xb_words", align_bytes=64)

from contextlib import ExitStack

import concourse.mybir as mybir

K, T, J, I, R, G, S = 512, 512, 256, 256, 512, 32, 32
FLOPS = 2 * K * R * J + 2 * K * R * I + 2 * R * J * I

F32 = mybir.dt.float32
BF16 = mybir.dt.bfloat16
I32 = mybir.dt.int32
U32 = mybir.dt.uint32
U16 = mybir.dt.uint16
U8 = mybir.dt.uint8
E4M3 = mybir.dt.float8_e4m3fn_x4
E5M2 = mybir.dt.float8_e5m2_x4
E2M1 = mybir.dt.float4_e2m1fn_x4
ALU = mybir.AluOpType

P = 128
PACK = 4
HALF = 128
RUN = 8


def load_scale_rows(queues, tile, scales):
    for quadrant, queue in enumerate(queues):
        queue.dma_start(
            out=tile[32 * quadrant : 32 * quadrant + 4, :].bitcast(I32),
            in_=scales[0, 4 * quadrant : 4 * quadrant + 4, :].bitcast(I32),
        )


def deal_columns(nc, dealt, raw, run):
    nc.scalar.copy(
        out=dealt.rearrange("p (t b q) -> p t b q", t=PACK, q=run),
        in_=raw.rearrange("p (b t q) -> p t b q", t=PACK, q=run),
    )


def tile_list_meet_lagged_levelled_bundlemax_kernel(
    tc, xt_words, xt_scales, wa_words, wa_scales, wb_words, wb_scales, bi, offs, offs2, out
):
    nc = tc.nc
    with ExitStack() as ctx:
        sb = ctx.enter_context(tc.tile_pool(name="sb", bufs=1))
        ps = ctx.enter_context(tc.psum_pool(name="ps", bufs=1))

        rows_list = sb.tile([P, J // 16], U16, name="rows_list")
        cols_list = sb.tile([P, I // 16], U16, name="cols_list")
        x_words = sb.tile([P, T], U32, name="x_words", align_bytes=64)
        x_scales = sb.tile([P, T], U8, name="x_scales", align_bytes=64)
        wa_raw = sb.tile([P, R], U16, name="wa_raw", align_bytes=64)
        wa_raw_scales = sb.tile([P, R], U8, name="wa_raw_scales", tag="wa_raw_scales", align_bytes=64)
        wb_raw = sb.tile([P, R], U32, name="wb_raw", align_bytes=64)
        wb_raw_scales = sb.tile([P, R], U8, name="wb_raw_scales", align_bytes=64)
        bias = sb.tile([P, I], F32, name="bias", align_bytes=64)
        za = sb.tile([P, (1 + J) * PACK], F32, name="za", align_bytes=64)

        nc.vector.memset(x_scales[:].bitcast(I32), 0)
        nc.vector.memset(wb_raw_scales[:].bitcast(I32), 0)
        nc.vector.memset(wa_raw_scales[:].bitcast(I32), 0)
        nc.vector.memset(za[:, 0:PACK], 0.0)

        nc.sync.dma_start(cols_list[:], offs2)
        nc.sync.dma_start(rows_list[:], offs)
        nc.sync.dma_start(out=x_words[:].bitcast(I32), in_=xt_words[0].rearrange("p n t -> p (n t)").bitcast(I32))
        load_scale_rows([nc.scalar] * 4, x_scales, xt_scales)
        nc.sync.dma_start(out=wb_raw[:].bitcast(I32), in_=wb_words[0].rearrange("p n t -> p (n t)").bitcast(I32))
        load_scale_rows([nc.sync, nc.sync, nc.sync, nc.gpsimd], wb_raw_scales, wb_scales)
        nc.sync.dma_start(out=wa_raw[:].bitcast(I32), in_=wa_words[0].bitcast(I32))
        load_scale_rows([nc.sync, nc.sync, nc.sync, nc.gpsimd], wa_raw_scales, wa_scales)
        nc.sync.dma_start(out=bias[:], in_=bi[0].partition_broadcast(P))

        xb_words = sb.tile([P, I], U32, name="xb_words", align_bytes=64)
        xb_scales = sb.tile([P, I], U8, name="xb_scales", align_bytes=64)
        xa_words = sb.tile([P, J], U32, name="xa_words", align_bytes=64)
        xa_scales = sb.tile([P, J], U8, name="xa_scales", align_bytes=64)
        nc.vector.tensor_copy(xb_words[:], x_words[:].indirect(cols_list[:]))
        nc.vector.tensor_copy(xb_scales[:], x_scales[:].indirect(cols_list[:]))
        nc.vector.tensor_copy(xa_words[:], x_words[:].indirect(rows_list[:]))
        nc.vector.tensor_copy(xa_scales[:], x_scales[:].indirect(rows_list[:]))

        wb_dealt = sb.tile([P, R], U32, name="wb_dealt", align_bytes=64)
        wb_dealt_scales = sb.tile([P, R], U8, name="wb_dealt_scales", align_bytes=64)
        wa_dealt = sb.tile([P, R], U16, name="wa_dealt", tag="wa_dealt", align_bytes=64)
        wa_dealt_scales = sb.tile([P, R], U8, name="wa_dealt_scales", align_bytes=64)
        deal_columns(nc, wb_dealt[:], wb_raw[:], RUN)
        deal_columns(nc, wb_dealt_scales[:].bitcast(U32), wb_raw_scales[:].bitcast(U32), RUN // 4)
        deal_columns(nc, wa_dealt[:].bitcast(U32), wa_raw[:].bitcast(U32), RUN // 2)
        deal_columns(nc, wa_dealt_scales[:].bitcast(U32), wa_raw_scales[:].bitcast(U32), RUN // 4)

        zb_banks = [ps.tile([P, PACK, HALF], F32, name="zb_bank%d" % h) for h in range(2)]
        za_banks = [ps.tile([P, PACK, HALF], F32, name="za_bank%d" % h) for h in range(2)]
        for h in range(2):
            cols = slice(h * HALF, (h + 1) * HALF)
            for t in range(PACK):
                feats = slice(t * P, (t + 1) * P)
                nc.tensor.matmul_mx(
                    out=zb_banks[h][:, t, :],
                    lhsT=wb_dealt[:, feats].bitcast(E5M2),
                    lhsT_scale=wb_dealt_scales[:, feats],
                    rhs=xb_words[:, cols].bitcast(E4M3),
                    rhs_scale=xb_scales[:, cols],
                    start=True,
                    stop=True,
                )
        bundles = HALF // RUN
        sums = [sb.tile([P, bundles, PACK], F32, name="sums%d" % h) for h in range(2)]
        means = [sb.tile([P, bundles, 1, PACK], F32, name="means%d" % h) for h in range(2)]
        hb = sb.tile([P, I * PACK], BF16, name="hb", align_bytes=64)
        ha = [sb.tile([P, HALF * PACK], BF16, name="ha%d" % h, align_bytes=64) for h in range(2)]
        for h in range(2):
            nc.vector.tensor_reduce(
                out=sums[h][:],
                in_=zb_banks[h][:].rearrange("p t (g m) -> p g t m", m=RUN),
                axis=mybir.AxisListType.X,
                op=ALU.add,
            )
        zb_late = sb.tile([P, HALF, PACK], F32, name="zb_late", tag="wa_raw_scales", align_bytes=64)
        nc.scalar.copy(out=zb_late[:], in_=zb_banks[0][:].rearrange("p t i -> p i t"))
        for h in range(2):
            rows = slice(h * HALF, (h + 1) * HALF)
            for t in range(PACK):
                feats = slice(t * P, (t + 1) * P)
                nc.tensor.matmul_mx(
                    out=za_banks[h][:, t, :],
                    lhsT=wa_dealt[:, feats].bitcast(E2M1),
                    lhsT_scale=wa_dealt_scales[:, feats],
                    rhs=xa_words[:, rows].bitcast(E4M3),
                    rhs_scale=xa_scales[:, rows],
                    start=True,
                    stop=True,
                )
            nc.scalar.copy(
                out=za[:, (1 + h * HALF) * PACK : (1 + (h + 1) * HALF) * PACK].rearrange("p (j t) -> p j t", t=PACK),
                in_=za_banks[h][:].rearrange("p t j -> p j t"),
            )

        scaled_bias = sb.tile([P, I], F32, name="scaled_bias", tag="wa_dealt", align_bytes=64)
        nc.scalar.activation(out=scaled_bias[:], in_=bias[:], func=mybir.ActivationFunctionType.Copy, scale=0.04)

        nc.gpsimd.tensor_scalar(means[0][:, :, 0, :], sums[0][:], 1.0 / RUN, 0.0, ALU.mult, ALU.add)
        nc.vector.tensor_scalar(means[1][:, :, 0, :], sums[1][:], 1.0 / RUN, None, ALU.mult)
        zb_views = [
            zb_late[:].rearrange("p (g m) t -> p g m t", m=RUN),
            zb_banks[1][:].rearrange("p t (g m) -> p g m t", m=RUN),
        ]

        def level(h, engine):
            engine.tensor_tensor(
                out=hb[:, h * HALF * PACK : (h + 1) * HALF * PACK].rearrange("p (g m t) -> p g m t", m=RUN, t=PACK),
                in0=zb_views[h],
                in1=means[h][:].broadcast_to([P, bundles, RUN, PACK]),
                op=ALU.subtract,
            )

        def lag(h):
            nc.vector.scalar_tensor_tensor(
                out=ha[h][:].rearrange("p (j t) -> p j t", t=PACK),
                in0=za[:, h * HALF * PACK : (h + 1) * HALF * PACK].rearrange("p (j t) -> p j t", t=PACK),
                scalar=-0.6,
                in1=za_banks[h][:].rearrange("p t j -> p j t"),
                op0=ALU.mult,
                op1=ALU.add,
            )

        hb_codes = sb.tile([P, I], U32, name="hb_codes", align_bytes=64)
        hb_scales = sb.tile([P, I], U8, name="hb_scales", align_bytes=64)
        ha_codes = [sb.tile([P, HALF], U32, name="ha_codes%d" % h, align_bytes=64) for h in range(2)]
        ha_scales = [sb.tile([P, HALF], U8, name="ha_scales%d" % h, align_bytes=64) for h in range(2)]
        a_banks = [ps.tile([P, I], F32, name="a_bank%d" % h) for h in range(2)]
        scores = [sb.tile([P, I], F32, name="scores%d" % h, align_bytes=64) for h in range(2)]
        best = [sb.tile([P, S], F32, name="best%d" % h, align_bytes=64) for h in range(2)]

        def quantize_rows(h):
            nc.vector.quantize_mx(out=ha_codes[h][:].bitcast(E4M3), scales=ha_scales[h][:], in_=ha[h][:])

        def meet(h):
            nc.tensor.matmul_mx(
                out=a_banks[h][:],
                lhsT=ha_codes[h][:].bitcast(E4M3),
                lhsT_scale=ha_scales[h][:],
                rhs=hb_codes[:].bitcast(E5M2),
                rhs_scale=hb_scales[:],
                start=True,
                stop=True,
            )

        def add_bias(h):
            nc.vector.scalar_tensor_tensor(
                out=scores[h][:], in0=a_banks[h][:], scalar=0.04, in1=scaled_bias[:], op0=ALU.mult, op1=ALU.add
            )

        def keep_best(h):
            nc.vector.tensor_reduce(
                out=best[h][:],
                in_=scores[h][:].rearrange("p (s m) -> p s m", m=I // S),
                axis=mybir.AxisListType.X,
                op=ALU.max,
            )
            nc.sync.dma_start(out=out[h * HALF : (h + 1) * HALF, :], in_=best[h][:])

        level(0, nc.gpsimd)
        lag(0)
        level(1, nc.vector)
        lag(1)
        quantize_rows(0)
        nc.vector.quantize_mx(out=hb_codes[:].bitcast(E5M2), scales=hb_scales[:], in_=hb[:])
        meet(0)
        quantize_rows(1)
        meet(1)
        add_bias(0)
        add_bias(1)
        keep_best(0)
        keep_best(1)
